import numpy as np
import ml_dtypes


def mxq(x, axis, fmt="e4m3"):
    dtype, down = {"e4m3": (ml_dtypes.float8_e4m3fn, 7), "e5m2": (ml_dtypes.float8_e5m2, 14)}[fmt]
    v = np.moveaxis(np.asarray(x, np.float32).astype(ml_dtypes.bfloat16).astype(np.float64), axis, -1)
    blocks = v.reshape(v.shape[:-1] + (-1, 32))
    amax = np.abs(blocks).max(-1, keepdims=True)
    byte = np.maximum(np.where(amax > 0, np.frexp(amax)[1] - 1 + 127, 0) - down, 1)
    scale = np.exp2(byte - 127.0)
    codes = (blocks / scale).astype(np.float32).astype(dtype).astype(np.float64)
    return np.moveaxis((codes * scale).reshape(v.shape), -1, axis)


WIDE = False


def mx_kscale(k):
    if not WIDE:
        return np.ones(k)
    levels = np.array([10, -10, 5, -5, 0])
    if k % 512:
        return np.exp2(np.random.permutation(np.resize(levels, k // 32))).repeat(32)
    a = np.empty((k // 512, 16))
    for p in range(k // 512):
        a[p, :8] = np.random.permutation(np.resize(levels, 8))
        for g in range(8):
            far = levels[np.abs(levels - a[p, g]) >= 10]
            a[p, g + 8] = far[np.random.randint(len(far))]
    return np.exp2(a.ravel()).repeat(32)


def f64(x):
    return np.asarray(x).astype(np.float64)


def striped(idx):
    return np.tile(idx.reshape(-1, 16).T, (8, 1)).astype(np.uint16)


def unstriped(offs):
    return offs[:16].T.reshape(-1).astype(np.int64)


def striped8(idx):
    return np.concatenate([x.reshape(-1, 16).T for x in idx]).astype(np.uint16)


def runs(offs, k):
    lists = np.stack([offs[16 * r : 16 * r + 16].T.reshape(-1) for r in range(8)]).astype(np.int64)
    return lists[np.arange(k) % 512 // 64]


def pack_weight(w):
    k, n = w.shape
    w = f64(np.asarray(w, np.float32).astype(ml_dtypes.bfloat16)).reshape(k // 32, 32, n)
    amax = np.abs(w).max(1)
    byte = np.clip(np.where(amax > 0, np.frexp(amax)[1] - 1 + 127 - 7, 1), 1, 254)
    scaled = (w * np.exp2(127.0 - byte)[:, None, :]).reshape(k, n).astype(np.float32)
    words = np.ascontiguousarray(scaled.reshape(k // 512, 128, 4, n).transpose(0, 1, 3, 2)).astype(ml_dtypes.float8_e4m3fn).view(np.uint8)
    return words, np.ascontiguousarray(byte.astype(np.uint8).reshape(k // 512, 16, n))


def unpack_weight(words, scales):
    g, p, n, _ = words.shape
    vals = np.ascontiguousarray(words).view(ml_dtypes.float8_e4m3fn).astype(np.float64) * np.repeat(np.exp2(scales.astype(np.float64) - 127.0), 8, axis=1)[..., None]
    return vals.transpose(0, 1, 3, 2).reshape(g * 512, n)


def relu(v):
    return np.maximum(v, 0.0)


K, T, S, N, H, U = 512, 2048, 512, 512, 512, 1024


def setup_inputs():
    n = np.random.standard_normal
    s = mx_kscale(K)[:, None]
    u = mx_kscale(S)
    packed_xT = pack_weight(n((K, T)) * s)
    return {
        "x_words": packed_xT[0],
        "x_scales": packed_xT[1],
        "wa": (n((K, H)) / np.sqrt(K) / s).astype(np.float32),
        "wb": (n((K, N)) / np.sqrt(K) / s).astype(np.float32),
        "gt": (np.random.uniform(0.5, 1.5, (S, 1)) * u[:, None]).astype(np.float32),
        "gi": (np.random.uniform(0.5, 1.5, (S, 1)) / u[:, None]).astype(np.float32),
        "offs": striped(np.random.permutation(T)[:S]),
        "two": striped(np.random.permutation(T)[:S]),
        "slot": striped8(np.stack([np.random.permutation(U)[:H] for _ in range(8)])),
    }


def reference(x_words, x_scales, wa, wb, gt, gi, offs, two, slot):
    xq = unpack_weight(x_words, x_scales)[:, unstriped(offs)]
    a = xq.T @ mxq(f64(wa), 0, "e4m3")
    ra = relu(a)
    pg = np.zeros((S, U))
    pg[np.arange(S)[:, None], runs(slot, S)] = ra
    z = f64(gt) * pg
    x_two = unpack_weight(x_words, x_scales)[:, unstriped(two)]
    b = x_two.T @ mxq(f64(wb), 0, "e4m3")
    z2 = f64(gi) * b
    cv = 0.0625 * ((mxq(z, 0, "e4m3").T @ mxq(z2, 0, "e4m3")))
    return cv

@@ -1,0 +1,231 @@
+from contextlib import ExitStack
+
+import concourse.mybir as mybir
+from concourse.masks import make_identity
+
+K, T, S, N, H, U = 512, 2048, 512, 512, 512, 1024
+FLOPS = 2 * K * S * H + 2 * K * S * N + 2 * S * U * N
+
+F32 = mybir.dt.float32
+BF16 = mybir.dt.bfloat16
+I32 = mybir.dt.int32
+U32 = mybir.dt.uint32
+U16 = mybir.dt.uint16
+U8 = mybir.dt.uint8
+FP8X4 = mybir.dt.float8_e4m3fn_x4
+COPY = mybir.ActivationFunctionType.Copy
+RELU = mybir.ActivationFunctionType.Relu
+MULT = mybir.AluOpType.mult
+
+P = 128
+PACK = 4
+RUN = 8
+HALF = 256
+CHUNKS = U // P
+WINDOWS = 3
+TAIL_GROUPS = ((0, 1), (1, 2), (2, 4), (4, 6), (6, 8))
+VECTOR_CHUNKS = (3, 5, 7)
+
+
+def tile_picked_momput2_none_p_kernel(
+    tc, x_words, x_scales, wa, wb, gt, gi, offs, two, slot, out
+):
+    nc = tc.nc
+    with ExitStack() as ctx:
+        keep = ctx.enter_context(tc.tile_pool(name="keep", bufs=1))
+        psum = ctx.enter_context(tc.psum_pool(name="psum", bufs=1))
+
+        def bank(tag="bank", bufs=6):
+            return psum.tile([P, 512], F32, name=tag, tag=tag, bufs=bufs)
+
+        offs_sb = keep.tile([P, S // 16], U16, name="offs_sb")
+        two_sb = keep.tile([P, S // 16], U16, name="two_sb")
+        slot_sb = keep.tile([P, H // 16], U16, name="slot_sb")
+        nc.sync.dma_start(offs_sb[:], offs)
+
+        table_scales = keep.tile([P, T], U8, name="table_scales", align_bytes=64)
+        nc.gpsimd.memset(table_scales[:].bitcast(I32), 0)
+        for q in range(4):
+            (nc.scalar if q < 2 else nc.sync).dma_start(
+                table_scales[32 * q : 32 * q + 4, :].bitcast(I32),
+                x_scales[0, 4 * q : 4 * q + 4, :].bitcast(I32),
+            )
+        nc.sync.dma_start(two_sb[:], two)
+        table_words = keep.tile([P, T], U32, name="table_words", align_bytes=64)
+        nc.sync.dma_start(
+            table_words[:].bitcast(I32),
+            x_words[0].rearrange("p n t -> p (n t)").bitcast(I32),
+        )
+
+        def load_half(w, h, name):
+            stage = keep.tile([P, PACK, HALF], F32, name=name)
+            rows = w.rearrange("(p j) n -> p j n", j=PACK)
+            nc.sync.dma_start(stage[:], rows[:, :, h * HALF : (h + 1) * HALF])
+            return stage
+
+        wa_stage = [load_half(wa, h, "wa_stage%d" % h) for h in range(2)]
+        nc.sync.dma_start(slot_sb[:], slot)
+
+        identity = keep.tile([P, P], F32, name="identity")
+        make_identity(nc, identity[:])
+        g_rows = keep.tile([P, P], F32, name="g_rows")
+        nc.gpsimd.memset(g_rows[:], 0.0)
+        for n, g in enumerate((gt, gi)):
+            nc.sync.dma_start(
+                g_rows[PACK * n : PACK * (n + 1), :].rearrange("t (q e) -> t q e", e=RUN),
+                g.rearrange("(q t e) o -> t q (e o)", t=PACK, e=RUN),
+            )
+        wb_stage = {h: load_half(wb, h, "wb_stage%d" % h) for h in (1, 0)}
+
+        windows = [keep.tile([P, U], F32, name="page%d" % i) for i in range(WINDOWS)]
+        nc.vector.memset(windows[0][:], 0.0)
+        for window in windows[1:]:
+            nc.scalar.activation(window[:], windows[0][:], COPY)
+
+        def gather_scales(idx, name):
+            listed = keep.tile([P, S], U8, name=name + "_listed", align_bytes=64)
+            nc.vector.tensor_copy(listed[:], table_scales[:].indirect(idx[:]))
+            dealt = keep.tile([P, S], U8, name=name + "_scales", align_bytes=64)
+            nc.vector.tensor_copy(
+                dealt[:].bitcast(I32).rearrange("p (t q e) -> p t q e", t=PACK, e=RUN // 4),
+                listed[:].bitcast(I32).rearrange("p (q t e) -> p t q e", t=PACK, e=RUN // 4),
+            )
+            return dealt
+
+        def gather_words(idx, name):
+            dealt = keep.tile([P, S], U32, name=name + "_words", align_bytes=64)
+            nc.vector.tensor_copy(
+                dealt[:].rearrange("p (t q e) -> p q t e", t=PACK, e=RUN),
+                table_words[:].indirect(idx[:]),
+            )
+            return dealt
+
+        xa_scales = gather_scales(offs_sb, "xa")
+        xb_scales = gather_scales(two_sb, "xb")
+        xa_words = gather_words(offs_sb, "xa")
+        xb_words = gather_words(two_sb, "xb")
+
+        def weight_tiles(name):
+            grouped = keep.tile([P, 512 * PACK], BF16, name=name + "_grouped", align_bytes=64)
+            codes = keep.tile([P, 512], U32, name=name + "_codes", align_bytes=64)
+            scales = keep.tile([P, 512], U8, name=name + "_qscales", align_bytes=64)
+            return grouped, codes, scales
+
+        def interleave_half(grouped, stage, h):
+            nc.scalar.activation(
+                grouped[:, h * HALF * PACK : (h + 1) * HALF * PACK].rearrange("p (c i j) -> p c j i", i=4, j=PACK),
+                stage[h][:].rearrange("p j (c i) -> p c j i", i=4),
+                COPY,
+            )
+
+        def quantize(grouped, codes, scales, lo, hi):
+            nc.vector.quantize_mx(
+                out=codes[:, lo:hi].bitcast(FP8X4),
+                scales=scales[:, lo:hi],
+                in_=grouped[:, lo * PACK : hi * PACK],
+            )
+
+        def product(acc, lhs_codes, lhs_scales, m, rhs_codes, rhs_scales, lo, hi):
+            nc.tensor.matmul_mx(
+                out=acc,
+                lhsT=lhs_codes[:, m * P : (m + 1) * P].bitcast(FP8X4),
+                lhsT_scale=lhs_scales[:, m * P : (m + 1) * P],
+                rhs=rhs_codes[:, lo:hi].bitcast(FP8X4),
+                rhs_scale=rhs_scales[:, lo:hi],
+                start=True,
+                stop=True,
+            )
+
+        wa_grouped, wa_codes, wa_scales = weight_tiles("wa")
+        wb_grouped = wa_grouped
+        wb_codes = keep.tile([P, 512], U32, name="wb_codes", align_bytes=64)
+        wb_scales = keep.tile([P, 512], U8, name="wb_qscales", align_bytes=64)
+        ra = {t: keep.tile([P, H], F32, name="ra%d" % t) for t in (0, 2)}
+        for h in range(2):
+            interleave_half(wa_grouped, wa_stage, h)
+            quantize(wa_grouped, wa_codes, wa_scales, h * HALF, (h + 1) * HALF)
+        for h in range(2):
+            cols = slice(h * HALF, (h + 1) * HALF)
+            acc = bank("shared", 1) if h == 1 else bank()
+            product(acc[:, :HALF], xa_words, xa_scales, 0, wa_codes, wa_scales, cols.start, cols.stop)
+            nc.scalar.activation(ra[0][:, cols], acc[:, :HALF], RELU)
+            nc.vector.tensor_copy(
+                windows[0][:].indirect(slot_sb[:, cols.start // 16 : cols.stop // 16]), ra[0][:, cols]
+            )
+
+        for h in (1, 0):
+            interleave_half(wb_grouped, wb_stage, h)
+        quantize(wb_grouped, wb_codes, wb_scales, 0, N)
+
+        spare = wb_stage[0][:].rearrange("p j n -> p (j n)")
+        sources = [None, spare[:, :H], ra[2][:], spare[:, :H]]
+
+        def project(t):
+            acc = bank("a", 1)
+            product(acc[:], xa_words, xa_scales, t, wa_codes, wa_scales, 0, H)
+            nc.scalar.activation(sources[t], acc[:], RELU)
+
+        project(1)
+        g_bank = bank("shared", 1)
+        nc.tensor.transpose(g_bank[:, :P], g_rows[:], identity[:])
+        g_cols = spare[:, H : H + 2 * PACK]
+        nc.scalar.activation(g_cols, g_bank[:, : 2 * PACK], COPY)
+        project(2)
+
+        z_pairs = keep.tile([P, 2 * U], U32, name="z_pairs", align_bytes=64)
+
+        def weigh_plane(t, c0, c1):
+            halves = z_pairs[:].bitcast(BF16).rearrange("p (c u n e) -> p c u n e", u=2, n=P, e=2)
+            nc.scalar.activation(
+                halves[:, c0:c1, t // 2, :, t % 2],
+                windows[t % WINDOWS][:, c0 * P : c1 * P].rearrange("p (c n) -> p c n", n=P),
+                COPY,
+                scale=g_cols[:, t : t + 1],
+            )
+
+        def scatter(t):
+            nc.vector.tensor_copy(windows[t % WINDOWS][:].indirect(slot_sb[:]), sources[t])
+
+        scatter(1)
+        weigh_plane(0, 0, CHUNKS)
+
+        z2_pairs = keep.tile([P, 2 * N], U32, name="z2_pairs", align_bytes=64)
+        z2_halves = z2_pairs[:].bitcast(BF16).rearrange("p (u n e) -> p u n e", u=2, e=2)
+        for t in range(PACK):
+            acc = bank()
+            product(acc[:], xb_words, xb_scales, t, wb_codes, wb_scales, 0, N)
+            nc.scalar.activation(
+                z2_halves[:, t // 2, :, t % 2], acc[:], COPY, scale=g_cols[:, PACK + t : PACK + t + 1]
+            )
+        scatter(2)
+        project(3)
+        weigh_plane(1, 0, CHUNKS)
+        z2_grouped, z2_codes, z2_scales = weight_tiles("z2")
+        nc.scalar.copy(
+            z2_grouped[:].bitcast(U32).rearrange("p (n u) -> p n u", u=2),
+            z2_pairs[:].rearrange("p (u n) -> p n u", u=2),
+        )
+        scatter(3)
+        weigh_plane(2, 0, CHUNKS)
+        quantize(z2_grouped, z2_codes, z2_scales, 0, N)
+
+        for c0, c1 in TAIL_GROUPS:
+            width = (c1 - c0) * P
+            weigh_plane(3, c0, c1)
+            grouped = keep.tile([P, width * PACK], BF16, name="z_grouped%d" % c0, align_bytes=64)
+            codes = keep.tile([P, width], U32, name="z_codes%d" % c0, align_bytes=64)
+            scales = keep.tile([P, width], U8, name="z_scales%d" % c0, align_bytes=64)
+            nc.vector.tensor_copy(
+                grouped[:].bitcast(I32).rearrange("p (c n u) -> p c n u", n=P, u=2),
+                z_pairs[:, 2 * c0 * P : 2 * c1 * P].bitcast(I32).rearrange("p (c u n) -> p c n u", u=2, n=P),
+            )
+            quantize(grouped, codes, scales, 0, width)
+            for c in range(c0, c1):
+                acc = bank()
+                product(acc[:], codes, scales, c - c0, z2_codes, z2_scales, 0, N)
+                result = keep.tile([P, N], F32, name="result%d" % c)
+                if c in VECTOR_CHUNKS:
+                    nc.vector.tensor_scalar(result[:], acc[:], 0.0625, None, MULT)
+                else:
+                    nc.scalar.activation(result[:], acc[:], COPY, scale=0.0625)
+                nc.sync.dma_start(out[c * P : (c + 1) * P, :], result[:])

@@ -23,8 +23,8 @@ RUN = 8
 HALF = 256
 CHUNKS = U // P
 WINDOWS = 3
-TAIL_GROUPS = ((0, 1), (1, 2), (2, 4), (4, 6), (6, 8))
-VECTOR_CHUNKS = (3, 5, 7)
+TAIL_GROUPS = ((0, 1), (1, 2), (2, 4), (4, 6), (6, 7), (7, 8))
+VECTOR_CHUNKS = (5, 7)
 
 
 def tile_picked_momput2_none_p_kernel(
@@ -42,15 +42,15 @@ def tile_picked_momput2_none_p_kernel(
         two_sb = keep.tile([P, S // 16], U16, name="two_sb")
         slot_sb = keep.tile([P, H // 16], U16, name="slot_sb")
         nc.sync.dma_start(offs_sb[:], offs)
+        nc.sync.dma_start(two_sb[:], two)
 
         table_scales = keep.tile([P, T], U8, name="table_scales", align_bytes=64)
-        nc.gpsimd.memset(table_scales[:].bitcast(I32), 0)
+        nc.vector.memset(table_scales[:].bitcast(I32), 0)
         for q in range(4):
             (nc.scalar if q < 2 else nc.sync).dma_start(
                 table_scales[32 * q : 32 * q + 4, :].bitcast(I32),
                 x_scales[0, 4 * q : 4 * q + 4, :].bitcast(I32),
             )
-        nc.sync.dma_start(two_sb[:], two)
         table_words = keep.tile([P, T], U32, name="table_words", align_bytes=64)
         nc.sync.dma_start(
             table_words[:].bitcast(I32),
@@ -92,18 +92,17 @@ def tile_picked_momput2_none_p_kernel(
             )
             return dealt
 
-        def gather_words(idx, name):
-            dealt = keep.tile([P, S], U32, name=name + "_words", align_bytes=64)
+        def gather_words(idx, dealt, lo, hi):
             nc.vector.tensor_copy(
-                dealt[:].rearrange("p (t q e) -> p q t e", t=PACK, e=RUN),
-                table_words[:].indirect(idx[:]),
+                dealt[:].rearrange("p (t q e) -> p q t e", t=PACK, e=RUN)[:, lo // 32 : hi // 32],
+                table_words[:].indirect(idx[:, lo // 16 : hi // 16]),
             )
-            return dealt
 
         xa_scales = gather_scales(offs_sb, "xa")
         xb_scales = gather_scales(two_sb, "xb")
-        xa_words = gather_words(offs_sb, "xa")
-        xb_words = gather_words(two_sb, "xb")
+        xa_words = keep.tile([P, S], U32, name="xa_words", align_bytes=64)
+        xb_words = keep.tile([P, S], U32, name="xb_words", align_bytes=64)
+        gather_words(offs_sb, xa_words, 0, S)
 
         def weight_tiles(name):
             grouped = keep.tile([P, 512 * PACK], BF16, name=name + "_grouped", align_bytes=64)
@@ -142,6 +141,7 @@ def tile_picked_momput2_none_p_kernel(
         wb_scales = keep.tile([P, 512], U8, name="wb_qscales", align_bytes=64)
         ra = {t: keep.tile([P, H], F32, name="ra%d" % t) for t in (0, 2)}
         for h in range(2):
+            gather_words(two_sb, xb_words, h * HALF, (h + 1) * HALF)
             interleave_half(wa_grouped, wa_stage, h)
             quantize(wa_grouped, wa_codes, wa_scales, h * HALF, (h + 1) * HALF)
         for h in range(2):
@@ -172,12 +172,11 @@ def tile_picked_momput2_none_p_kernel(
         nc.scalar.activation(g_cols, g_bank[:, : 2 * PACK], COPY)
         project(2)
 
-        z_pairs = keep.tile([P, 2 * U], U32, name="z_pairs", align_bytes=64)
+        z_planes = keep.tile([P, PACK * U], BF16, name="z_planes", align_bytes=64)
 
         def weigh_plane(t, c0, c1):
-            halves = z_pairs[:].bitcast(BF16).rearrange("p (c u n e) -> p c u n e", u=2, n=P, e=2)
             nc.scalar.activation(
-                halves[:, c0:c1, t // 2, :, t % 2],
+                z_planes[:].rearrange("p (c t n) -> p c t n", t=PACK, n=P)[:, c0:c1, t, :],
                 windows[t % WINDOWS][:, c0 * P : c1 * P].rearrange("p (c n) -> p c n", n=P),
                 COPY,
                 scale=g_cols[:, t : t + 1],
@@ -189,37 +188,46 @@ def tile_picked_momput2_none_p_kernel(
         scatter(1)
         weigh_plane(0, 0, CHUNKS)
 
-        z2_pairs = keep.tile([P, 2 * N], U32, name="z2_pairs", align_bytes=64)
-        z2_halves = z2_pairs[:].bitcast(BF16).rearrange("p (u n e) -> p u n e", u=2, e=2)
+        z2_planes = keep.tile([P, PACK, N], BF16, name="z2_planes", align_bytes=64)
         for t in range(PACK):
             acc = bank()
             product(acc[:], xb_words, xb_scales, t, wb_codes, wb_scales, 0, N)
             nc.scalar.activation(
-                z2_halves[:, t // 2, :, t % 2], acc[:], COPY, scale=g_cols[:, PACK + t : PACK + t + 1]
+                z2_planes[:, t, :], acc[:], COPY, scale=g_cols[:, PACK + t : PACK + t + 1]
             )
         scatter(2)
         project(3)
         weigh_plane(1, 0, CHUNKS)
         z2_grouped, z2_codes, z2_scales = weight_tiles("z2")
         nc.scalar.copy(
-            z2_grouped[:].bitcast(U32).rearrange("p (n u) -> p n u", u=2),
-            z2_pairs[:].rearrange("p (u n) -> p n u", u=2),
+            z2_grouped[:].rearrange("p (n i t) -> p n t i", i=4, t=PACK),
+            z2_planes[:].rearrange("p t (n i) -> p n t i", i=4),
         )
         scatter(3)
         weigh_plane(2, 0, CHUNKS)
-        quantize(z2_grouped, z2_codes, z2_scales, 0, N)
+        z_tiles = []
 
-        for c0, c1 in TAIL_GROUPS:
+        def interleave_group(c0, c1):
             width = (c1 - c0) * P
             weigh_plane(3, c0, c1)
             grouped = keep.tile([P, width * PACK], BF16, name="z_grouped%d" % c0, align_bytes=64)
             codes = keep.tile([P, width], U32, name="z_codes%d" % c0, align_bytes=64)
             scales = keep.tile([P, width], U8, name="z_scales%d" % c0, align_bytes=64)
             nc.vector.tensor_copy(
-                grouped[:].bitcast(I32).rearrange("p (c n u) -> p c n u", n=P, u=2),
-                z_pairs[:, 2 * c0 * P : 2 * c1 * P].bitcast(I32).rearrange("p (c u n) -> p c n u", u=2, n=P),
+                grouped[:].rearrange("p (c n i t) -> p c n t i", n=P // 4, i=4, t=PACK),
+                z_planes[:, PACK * c0 * P : PACK * c1 * P].rearrange("p (c t n i) -> p c n t i", t=PACK, n=P // 4, i=4),
             )
-            quantize(grouped, codes, scales, 0, width)
+            z_tiles.append((grouped, codes, scales, 0, width))
+
+        quantize(z2_grouped, z2_codes, z2_scales, 0, N)
+        interleave_group(*TAIL_GROUPS[0])
+        for i in range(len(TAIL_GROUPS)):
+            if i + 1 < len(TAIL_GROUPS):
+                interleave_group(*TAIL_GROUPS[i + 1])
+            quantize(*z_tiles[i])
+
+        for (c0, c1), tiles in zip(TAIL_GROUPS, z_tiles):
+            codes, scales = tiles[1], tiles[2]
             for c in range(c0, c1):
                 acc = bank()
                 product(acc[:], codes, scales, c - c0, z2_codes, z2_scales, 0, N)

@@ -20,11 +20,16 @@ MULT = mybir.AluOpType.mult
 P = 128
 PACK = 4
 RUN = 8
-HALF = 256
+NEAR = 4
+PER_COLUMN = 16
+BANK = 512
+OUT_SCALE = 0.0625
+
+LOWER, UPPER = (0, 256), (256, 512)
 CHUNKS = U // P
-WINDOWS = 3
-TAIL_GROUPS = ((0, 1), (1, 2), (2, 4), (4, 6), (6, 7), (7, 8))
-VECTOR_CHUNKS = (5, 7)
+TAIL_GROUPS = ((0, 1), (1, 2), (2, 4), (4, 6), (6, 8))
+SPLIT_CHUNKS = (0, CHUNKS - 1)
+VECTOR_PIECES = ((CHUNKS - 2, 0), (CHUNKS - 1, UPPER[0]))
 
 
 def tile_picked_momput2_none_p_kernel(
@@ -35,12 +40,22 @@ def tile_picked_momput2_none_p_kernel(
         keep = ctx.enter_context(tc.tile_pool(name="keep", bufs=1))
         psum = ctx.enter_context(tc.psum_pool(name="psum", bufs=1))
 
-        def bank(tag="bank", bufs=6):
-            return psum.tile([P, 512], F32, name=tag, tag=tag, bufs=bufs)
+        def ring_bank():
+            return psum.tile([P, BANK], F32, name="ring", tag="ring", bufs=7)
 
-        offs_sb = keep.tile([P, S // 16], U16, name="offs_sb")
-        two_sb = keep.tile([P, S // 16], U16, name="two_sb")
-        slot_sb = keep.tile([P, H // 16], U16, name="slot_sb")
+        def eighth_bank():
+            return psum.tile([P, BANK], F32, name="eighth", tag="eighth", bufs=1)
+
+        offs_sb = keep.tile([P, S // PER_COLUMN], U16, name="offs_sb")
+        two_sb = keep.tile([P, S // PER_COLUMN], U16, name="two_sb")
+        slot_sb = keep.tile([P, H // PER_COLUMN], U16, name="slot_sb")
+
+        def load_half(w, cols, name):
+            lo, hi = cols
+            stage = keep.tile([P, PACK, hi - lo], F32, name="%s_stage%d" % (name, lo))
+            nc.sync.dma_start(stage[:], w.rearrange("(p j) n -> p j n", j=PACK)[:, :, lo:hi])
+            return stage[:]
+
         nc.sync.dma_start(offs_sb[:], offs)
         nc.sync.dma_start(two_sb[:], two)
 
@@ -51,189 +66,200 @@ def tile_picked_momput2_none_p_kernel(
                 table_scales[32 * q : 32 * q + 4, :].bitcast(I32),
                 x_scales[0, 4 * q : 4 * q + 4, :].bitcast(I32),
             )
+        wa_stage = {LOWER: load_half(wa, LOWER, "wa")}
         table_words = keep.tile([P, T], U32, name="table_words", align_bytes=64)
         nc.sync.dma_start(
             table_words[:].bitcast(I32),
             x_words[0].rearrange("p n t -> p (n t)").bitcast(I32),
         )
-
-        def load_half(w, h, name):
-            stage = keep.tile([P, PACK, HALF], F32, name=name)
-            rows = w.rearrange("(p j) n -> p j n", j=PACK)
-            nc.sync.dma_start(stage[:], rows[:, :, h * HALF : (h + 1) * HALF])
-            return stage
-
-        wa_stage = [load_half(wa, h, "wa_stage%d" % h) for h in range(2)]
+        wa_stage[UPPER] = load_half(wa, UPPER, "wa")
         nc.sync.dma_start(slot_sb[:], slot)
 
         identity = keep.tile([P, P], F32, name="identity")
         make_identity(nc, identity[:])
-        g_rows = keep.tile([P, P], F32, name="g_rows")
-        nc.gpsimd.memset(g_rows[:], 0.0)
-        for n, g in enumerate((gt, gi)):
+        gain_rows = keep.tile([P, P], F32, name="gain_rows")
+        nc.gpsimd.memset(gain_rows[:], 0.0)
+        for n, gain in enumerate((gt, gi)):
             nc.sync.dma_start(
-                g_rows[PACK * n : PACK * (n + 1), :].rearrange("t (q e) -> t q e", e=RUN),
-                g.rearrange("(q t e) o -> t q (e o)", t=PACK, e=RUN),
+                gain_rows[PACK * n : PACK * (n + 1), :].rearrange("t (q e) -> t q e", e=RUN),
+                gain.rearrange("(q t e) o -> t q (e o)", t=PACK, e=RUN),
             )
-        wb_stage = {h: load_half(wb, h, "wb_stage%d" % h) for h in (1, 0)}
+        wb_stage = {cols: load_half(wb, cols, "wb") for cols in (UPPER, LOWER)}
 
-        windows = [keep.tile([P, U], F32, name="page%d" % i) for i in range(WINDOWS)]
-        nc.vector.memset(windows[0][:], 0.0)
-        for window in windows[1:]:
-            nc.scalar.activation(window[:], windows[0][:], COPY)
+        pages = [keep.tile([P, U], F32, name="page%d" % n) for n in range(2)]
+        nc.vector.memset(pages[0][:], 0.0)
+        nc.scalar.activation(pages[1][:], pages[0][:], COPY)
 
-        def gather_scales(idx, name):
-            listed = keep.tile([P, S], U8, name=name + "_listed", align_bytes=64)
-            nc.vector.tensor_copy(listed[:], table_scales[:].indirect(idx[:]))
-            dealt = keep.tile([P, S], U8, name=name + "_scales", align_bytes=64)
-            nc.vector.tensor_copy(
-                dealt[:].bitcast(I32).rearrange("p (t q e) -> p t q e", t=PACK, e=RUN // 4),
-                listed[:].bitcast(I32).rearrange("p (q t e) -> p t q e", t=PACK, e=RUN // 4),
-            )
-            return dealt
-
-        def gather_words(idx, dealt, lo, hi):
-            nc.vector.tensor_copy(
-                dealt[:].rearrange("p (t q e) -> p q t e", t=PACK, e=RUN)[:, lo // 32 : hi // 32],
-                table_words[:].indirect(idx[:, lo // 16 : hi // 16]),
-            )
-
-        xa_scales = gather_scales(offs_sb, "xa")
-        xb_scales = gather_scales(two_sb, "xb")
+        listed_scales = keep.tile([P, 2 * S], U8, name="listed_scales", align_bytes=64)
+        for n, idx in enumerate((offs_sb, two_sb)):
+            nc.vector.tensor_copy(listed_scales[:, n * S : (n + 1) * S], table_scales[:].indirect(idx[:]))
+        dealt_scales = keep.tile([P, 2 * S], U8, name="dealt_scales", align_bytes=64)
         xa_words = keep.tile([P, S], U32, name="xa_words", align_bytes=64)
         xb_words = keep.tile([P, S], U32, name="xb_words", align_bytes=64)
-        gather_words(offs_sb, xa_words, 0, S)
+        xa = (xa_words, dealt_scales[:, :S])
+        xb = (xb_words, dealt_scales[:, S:])
 
-        def weight_tiles(name):
-            grouped = keep.tile([P, 512 * PACK], BF16, name=name + "_grouped", align_bytes=64)
-            codes = keep.tile([P, 512], U32, name=name + "_codes", align_bytes=64)
-            scales = keep.tile([P, 512], U8, name=name + "_qscales", align_bytes=64)
-            return grouped, codes, scales
-
-        def interleave_half(grouped, stage, h):
-            nc.scalar.activation(
-                grouped[:, h * HALF * PACK : (h + 1) * HALF * PACK].rearrange("p (c i j) -> p c j i", i=4, j=PACK),
-                stage[h][:].rearrange("p j (c i) -> p c j i", i=4),
-                COPY,
+        def deal_scales():
+            nc.vector.tensor_copy(
+                dealt_scales[:].bitcast(I32).rearrange("p (n t q e) -> p n t q e", n=2, t=PACK, e=RUN // 4),
+                listed_scales[:].bitcast(I32).rearrange("p (n q t e) -> p n t q e", n=2, t=PACK, e=RUN // 4),
             )
 
-        def quantize(grouped, codes, scales, lo, hi):
+        def gather_words(idx, words):
+            nc.vector.tensor_copy(
+                words[:].rearrange("p (t q e) -> p q t e", t=PACK, e=RUN),
+                table_words[:].indirect(idx[:]),
+            )
+
+        def mx_operand(name, width):
+            codes = keep.tile([P, width], U32, name=name + "_codes", align_bytes=64)
+            scales = keep.tile([P, width], U8, name=name + "_scales", align_bytes=64)
+            return codes, scales
+
+        def grouped_tile(name, width):
+            return keep.tile([P, width * PACK], BF16, name=name + "_grouped", align_bytes=64)
+
+        def grouped_view(grouped, cols):
+            lo, hi = cols
+            return grouped[:, lo * PACK : hi * PACK].rearrange("p (c i j) -> p c j i", i=NEAR, j=PACK)
+
+        def quantize(operand, grouped, cols):
+            lo, hi = cols
             nc.vector.quantize_mx(
-                out=codes[:, lo:hi].bitcast(FP8X4),
-                scales=scales[:, lo:hi],
+                out=operand[0][:, lo:hi].bitcast(FP8X4),
+                scales=operand[1][:, lo:hi],
                 in_=grouped[:, lo * PACK : hi * PACK],
             )
 
-        def product(acc, lhs_codes, lhs_scales, m, rhs_codes, rhs_scales, lo, hi):
+        def product(bank, stationary, m, moving, cols):
+            lo, hi = cols
+            acc = bank[:, : hi - lo]
             nc.tensor.matmul_mx(
                 out=acc,
-                lhsT=lhs_codes[:, m * P : (m + 1) * P].bitcast(FP8X4),
-                lhsT_scale=lhs_scales[:, m * P : (m + 1) * P],
-                rhs=rhs_codes[:, lo:hi].bitcast(FP8X4),
-                rhs_scale=rhs_scales[:, lo:hi],
+                lhsT=stationary[0][:, m * P : (m + 1) * P].bitcast(FP8X4),
+                lhsT_scale=stationary[1][:, m * P : (m + 1) * P],
+                rhs=moving[0][:, lo:hi].bitcast(FP8X4),
+                rhs_scale=moving[1][:, lo:hi],
                 start=True,
                 stop=True,
             )
+            return acc
 
-        wa_grouped, wa_codes, wa_scales = weight_tiles("wa")
-        wb_grouped = wa_grouped
-        wb_codes = keep.tile([P, 512], U32, name="wb_codes", align_bytes=64)
-        wb_scales = keep.tile([P, 512], U8, name="wb_qscales", align_bytes=64)
-        ra = {t: keep.tile([P, H], F32, name="ra%d" % t) for t in (0, 2)}
-        for h in range(2):
-            gather_words(two_sb, xb_words, h * HALF, (h + 1) * HALF)
-            interleave_half(wa_grouped, wa_stage, h)
-            quantize(wa_grouped, wa_codes, wa_scales, h * HALF, (h + 1) * HALF)
-        for h in range(2):
-            cols = slice(h * HALF, (h + 1) * HALF)
-            acc = bank("shared", 1) if h == 1 else bank()
-            product(acc[:, :HALF], xa_words, xa_scales, 0, wa_codes, wa_scales, cols.start, cols.stop)
-            nc.scalar.activation(ra[0][:, cols], acc[:, :HALF], RELU)
-            nc.vector.tensor_copy(
-                windows[0][:].indirect(slot_sb[:, cols.start // 16 : cols.stop // 16]), ra[0][:, cols]
-            )
+        w_grouped = grouped_tile("w", H)
+        wa_mx = mx_operand("wa", H)
+        wb_mx = mx_operand("wb", N)
 
-        for h in (1, 0):
-            interleave_half(wb_grouped, wb_stage, h)
-        quantize(wb_grouped, wb_codes, wb_scales, 0, N)
+        def interleave_weights(stage, cols):
+            rows = stage[cols].rearrange("p j (c i) -> p c j i", i=NEAR)
+            nc.scalar.activation(grouped_view(w_grouped, cols), rows, COPY)
 
-        spare = wb_stage[0][:].rearrange("p j n -> p (j n)")
-        sources = [None, spare[:, :H], ra[2][:], spare[:, :H]]
+        def freed(stage, start):
+            return stage.rearrange("p j n -> p (j n)")[:, start : start + H]
 
-        def project(t):
-            acc = bank("a", 1)
-            product(acc[:], xa_words, xa_scales, t, wa_codes, wa_scales, 0, H)
-            nc.scalar.activation(sources[t], acc[:], RELU)
+        ra = [
+            freed(wa_stage[UPPER], 0),
+            freed(wb_stage[UPPER], 0),
+            freed(wb_stage[UPPER], H),
+            freed(wb_stage[LOWER], H),
+        ]
 
-        project(1)
-        g_bank = bank("shared", 1)
-        nc.tensor.transpose(g_bank[:, :P], g_rows[:], identity[:])
-        g_cols = spare[:, H : H + 2 * PACK]
-        nc.scalar.activation(g_cols, g_bank[:, : 2 * PACK], COPY)
-        project(2)
+        def project(t, cols, bank):
+            lo, hi = cols
+            nc.scalar.activation(ra[t][:, lo:hi], product(bank, xa, t, wa_mx, cols), RELU)
 
-        z_planes = keep.tile([P, PACK * U], BF16, name="z_planes", align_bytes=64)
+        def scatter(t, cols):
+            lo, hi = cols
+            entries = slot_sb[:, lo // PER_COLUMN : hi // PER_COLUMN]
+            nc.vector.tensor_copy(pages[t % 2][:].indirect(entries), ra[t][:, lo:hi])
 
-        def weigh_plane(t, c0, c1):
+        interleave_weights(wa_stage, LOWER)
+        quantize(wa_mx, w_grouped, LOWER)
+        deal_scales()
+        gather_words(offs_sb, xa_words)
+        gather_words(two_sb, xb_words)
+        interleave_weights(wa_stage, UPPER)
+        quantize(wa_mx, w_grouped, UPPER)
+        project(0, LOWER, ring_bank())
+        scatter(0, LOWER)
+        project(0, UPPER, eighth_bank())
+        interleave_weights(wb_stage, UPPER)
+        quantize(wb_mx, w_grouped, UPPER)
+        project(1, (0, H), ring_bank())
+        scatter(0, UPPER)
+        interleave_weights(wb_stage, LOWER)
+        for t in range(2, PACK):
+            project(t, (0, H), ring_bank())
+
+        turned = eighth_bank()
+        nc.tensor.transpose(turned[:, :P], gain_rows[:], identity[:])
+        gains = wb_stage[LOWER][:, 0, : 2 * PACK]
+        nc.scalar.activation(gains, turned[:, : 2 * PACK], COPY)
+
+        z_rows = keep.tile([P, PACK * U], BF16, name="z_rows", align_bytes=64)
+
+        def weigh_page(t, c0, c1):
             nc.scalar.activation(
-                z_planes[:].rearrange("p (c t n) -> p c t n", t=PACK, n=P)[:, c0:c1, t, :],
-                windows[t % WINDOWS][:, c0 * P : c1 * P].rearrange("p (c n) -> p c n", n=P),
+                z_rows[:].rearrange("p (c t n) -> p c t n", t=PACK, n=P)[:, c0:c1, t, :],
+                pages[t % 2][:, c0 * P : c1 * P].rearrange("p (c n) -> p c n", n=P),
                 COPY,
-                scale=g_cols[:, t : t + 1],
+                scale=gains[:, t : t + 1],
             )
 
-        def scatter(t):
-            nc.vector.tensor_copy(windows[t % WINDOWS][:].indirect(slot_sb[:]), sources[t])
+        z2_grouped = grouped_tile("z2", N)
+        z2_mx = mx_operand("z2", N)
 
-        scatter(1)
-        weigh_plane(0, 0, CHUNKS)
+        def make_z2(cols):
+            lo, hi = cols
+            rows = keep.tile([P, PACK, hi - lo], BF16, name="z2_rows%d" % lo, align_bytes=64)
+            for t in range(PACK):
+                acc = product(ring_bank(), xb, t, wb_mx, cols)
+                nc.scalar.activation(rows[:, t, :], acc, COPY, scale=gains[:, PACK + t : PACK + t + 1])
+            nc.scalar.copy(grouped_view(z2_grouped, cols), rows[:].rearrange("p t (c i) -> p c t i", i=NEAR))
 
-        z2_planes = keep.tile([P, PACK, N], BF16, name="z2_planes", align_bytes=64)
-        for t in range(PACK):
-            acc = bank()
-            product(acc[:], xb_words, xb_scales, t, wb_codes, wb_scales, 0, N)
-            nc.scalar.activation(
-                z2_planes[:, t, :], acc[:], COPY, scale=g_cols[:, PACK + t : PACK + t + 1]
-            )
-        scatter(2)
-        project(3)
-        weigh_plane(1, 0, CHUNKS)
-        z2_grouped, z2_codes, z2_scales = weight_tiles("z2")
-        nc.scalar.copy(
-            z2_grouped[:].rearrange("p (n i t) -> p n t i", i=4, t=PACK),
-            z2_planes[:].rearrange("p t (n i) -> p n t i", i=4),
-        )
-        scatter(3)
-        weigh_plane(2, 0, CHUNKS)
-        z_tiles = []
+        scatter(1, (0, H))
+        quantize(wb_mx, w_grouped, LOWER)
+        weigh_page(0, 0, CHUNKS)
+        make_z2(UPPER)
+        scatter(2, (0, H))
+        weigh_page(1, 0, CHUNKS)
+        make_z2(LOWER)
+        scatter(3, (0, H))
+        weigh_page(2, 0, CHUNKS)
 
-        def interleave_group(c0, c1):
-            width = (c1 - c0) * P
-            weigh_plane(3, c0, c1)
-            grouped = keep.tile([P, width * PACK], BF16, name="z_grouped%d" % c0, align_bytes=64)
-            codes = keep.tile([P, width], U32, name="z_codes%d" % c0, align_bytes=64)
-            scales = keep.tile([P, width], U8, name="z_scales%d" % c0, align_bytes=64)
+        z_grouped, z_mx = {}, {}
+
+        def interleave_z(group):
+            c0, c1 = group
+            weigh_page(PACK - 1, c0, c1)
+            z_grouped[group] = grouped_tile("z_from%d" % c0, (c1 - c0) * P)
+            z_mx[group] = mx_operand("z_from%d" % c0, (c1 - c0) * P)
             nc.vector.tensor_copy(
-                grouped[:].rearrange("p (c n i t) -> p c n t i", n=P // 4, i=4, t=PACK),
-                z_planes[:, PACK * c0 * P : PACK * c1 * P].rearrange("p (c t n i) -> p c n t i", t=PACK, n=P // 4, i=4),
+                z_grouped[group][:].rearrange("p (c n i t) -> p c n t i", n=P // NEAR, i=NEAR, t=PACK),
+                z_rows[:, PACK * c0 * P : PACK * c1 * P].rearrange(
+                    "p (c t n i) -> p c n t i", t=PACK, n=P // NEAR, i=NEAR
+                ),
             )
-            z_tiles.append((grouped, codes, scales, 0, width))
 
-        quantize(z2_grouped, z2_codes, z2_scales, 0, N)
-        interleave_group(*TAIL_GROUPS[0])
-        for i in range(len(TAIL_GROUPS)):
-            if i + 1 < len(TAIL_GROUPS):
-                interleave_group(*TAIL_GROUPS[i + 1])
-            quantize(*z_tiles[i])
+        def quantize_z(group):
+            quantize(z_mx[group], z_grouped[group], (0, (group[1] - group[0]) * P))
 
-        for (c0, c1), tiles in zip(TAIL_GROUPS, z_tiles):
-            codes, scales = tiles[1], tiles[2]
-            for c in range(c0, c1):
-                acc = bank()
-                product(acc[:], codes, scales, c - c0, z2_codes, z2_scales, 0, N)
-                result = keep.tile([P, N], F32, name="result%d" % c)
-                if c in VECTOR_CHUNKS:
-                    nc.vector.tensor_scalar(result[:], acc[:], 0.0625, None, MULT)
-                else:
-                    nc.scalar.activation(result[:], acc[:], COPY, scale=0.0625)
-                nc.sync.dma_start(out[c * P : (c + 1) * P, :], result[:])
+        quantize(z2_mx, z2_grouped, UPPER)
+        interleave_z(TAIL_GROUPS[0])
+        quantize(z2_mx, z2_grouped, LOWER)
+        quantize_z(TAIL_GROUPS[0])
+        interleave_z(TAIL_GROUPS[1])
+        for group, following in zip(TAIL_GROUPS[1:], TAIL_GROUPS[2:]):
+            interleave_z(following)
+            quantize_z(group)
+        quantize_z(TAIL_GROUPS[-1])
+
+        for group in TAIL_GROUPS:
+            for c in range(*group):
+                for lo, hi in (LOWER, UPPER) if c in SPLIT_CHUNKS else ((0, N),):
+                    acc = product(ring_bank(), z_mx[group], c - group[0], z2_mx, (lo, hi))
+                    result = keep.tile([P, hi - lo], F32, name="result%d_%d" % (c, lo))
+                    if (c, lo) in VECTOR_PIECES:
+                        nc.vector.tensor_scalar(result[:], acc, OUT_SCALE, None, MULT)
+                    else:
+                        nc.scalar.activation(result[:], acc, COPY, scale=OUT_SCALE)
+                    nc.sync.dma_start(out[c * P : (c + 1) * P, lo:hi], result[:])

from contextlib import ExitStack

import concourse.mybir as mybir
from concourse.masks import make_identity

K, T, S, N, H, U = 512, 2048, 512, 512, 512, 1024
FLOPS = 2 * K * S * H + 2 * K * S * N + 2 * S * U * N

F32 = mybir.dt.float32
BF16 = mybir.dt.bfloat16
I32 = mybir.dt.int32
U32 = mybir.dt.uint32
U16 = mybir.dt.uint16
U8 = mybir.dt.uint8
FP8X4 = mybir.dt.float8_e4m3fn_x4
COPY = mybir.ActivationFunctionType.Copy
RELU = mybir.ActivationFunctionType.Relu
MULT = mybir.AluOpType.mult

P = 128
PACK = 4
RUN = 8
NEAR = 4
PER_COLUMN = 16
BANK = 512
OUT_SCALE = 0.0625

LOWER, UPPER = (0, 256), (256, 512)
CHUNKS = U // P
TAIL_GROUPS = ((0, 1), (1, 2), (2, 4), (4, 6), (6, 8))
SPLIT_CHUNKS = (0, CHUNKS - 1)
VECTOR_PIECES = ((CHUNKS - 2, 0), (CHUNKS - 1, UPPER[0]))


def tile_picked_momput2_none_p_kernel(
    tc, x_words, x_scales, wa, wb, gt, gi, offs, two, slot, out
):
    nc = tc.nc
    with ExitStack() as ctx:
        keep = ctx.enter_context(tc.tile_pool(name="keep", bufs=1))
        psum = ctx.enter_context(tc.psum_pool(name="psum", bufs=1))

        def ring_bank():
            return psum.tile([P, BANK], F32, name="ring", tag="ring", bufs=7)

        def eighth_bank():
            return psum.tile([P, BANK], F32, name="eighth", tag="eighth", bufs=1)

        offs_sb = keep.tile([P, S // PER_COLUMN], U16, name="offs_sb")
        two_sb = keep.tile([P, S // PER_COLUMN], U16, name="two_sb")
        slot_sb = keep.tile([P, H // PER_COLUMN], U16, name="slot_sb")

        def load_half(w, cols, name):
            lo, hi = cols
            stage = keep.tile([P, PACK, hi - lo], F32, name="%s_stage%d" % (name, lo))
            nc.sync.dma_start(stage[:], w.rearrange("(p j) n -> p j n", j=PACK)[:, :, lo:hi])
            return stage[:]

        nc.sync.dma_start(offs_sb[:], offs)
        nc.sync.dma_start(two_sb[:], two)

        table_scales = keep.tile([P, T], U8, name="table_scales", align_bytes=64)
        nc.vector.memset(table_scales[:].bitcast(I32), 0)
        for q in range(4):
            (nc.scalar if q < 2 else nc.sync).dma_start(
                table_scales[32 * q : 32 * q + 4, :].bitcast(I32),
                x_scales[0, 4 * q : 4 * q + 4, :].bitcast(I32),
            )
        wa_stage = {LOWER: load_half(wa, LOWER, "wa")}
        table_words = keep.tile([P, T], U32, name="table_words", align_bytes=64)
        nc.sync.dma_start(
            table_words[:].bitcast(I32),
            x_words[0].rearrange("p n t -> p (n t)").bitcast(I32),
        )
        wa_stage[UPPER] = load_half(wa, UPPER, "wa")
        nc.sync.dma_start(slot_sb[:], slot)

        identity = keep.tile([P, P], F32, name="identity")
        make_identity(nc, identity[:])
        gain_rows = keep.tile([P, P], F32, name="gain_rows")
        nc.gpsimd.memset(gain_rows[:], 0.0)
        for n, gain in enumerate((gt, gi)):
            nc.sync.dma_start(
                gain_rows[PACK * n : PACK * (n + 1), :].rearrange("t (q e) -> t q e", e=RUN),
                gain.rearrange("(q t e) o -> t q (e o)", t=PACK, e=RUN),
            )
        wb_stage = {cols: load_half(wb, cols, "wb") for cols in (UPPER, LOWER)}

        pages = [keep.tile([P, U], F32, name="page%d" % n) for n in range(2)]
        nc.vector.memset(pages[0][:], 0.0)
        nc.scalar.activation(pages[1][:], pages[0][:], COPY)

        listed_scales = keep.tile([P, 2 * S], U8, name="listed_scales", align_bytes=64)
        for n, idx in enumerate((offs_sb, two_sb)):
            nc.vector.tensor_copy(listed_scales[:, n * S : (n + 1) * S], table_scales[:].indirect(idx[:]))
        dealt_scales = keep.tile([P, 2 * S], U8, name="dealt_scales", align_bytes=64)
        xa_words = keep.tile([P, S], U32, name="xa_words", align_bytes=64)
        xb_words = keep.tile([P, S], U32, name="xb_words", align_bytes=64)
        xa = (xa_words, dealt_scales[:, :S])
        xb = (xb_words, dealt_scales[:, S:])

        def deal_scales():
            nc.vector.tensor_copy(
                dealt_scales[:].bitcast(I32).rearrange("p (n t q e) -> p n t q e", n=2, t=PACK, e=RUN // 4),
                listed_scales[:].bitcast(I32).rearrange("p (n q t e) -> p n t q e", n=2, t=PACK, e=RUN // 4),
            )

        def gather_words(idx, words):
            nc.vector.tensor_copy(
                words[:].rearrange("p (t q e) -> p q t e", t=PACK, e=RUN),
                table_words[:].indirect(idx[:]),
            )

        def mx_operand(name, width):
            codes = keep.tile([P, width], U32, name=name + "_codes", align_bytes=64)
            scales = keep.tile([P, width], U8, name=name + "_scales", align_bytes=64)
            return codes, scales

        def grouped_tile(name, width):
            return keep.tile([P, width * PACK], BF16, name=name + "_grouped", align_bytes=64)

        def grouped_view(grouped, cols):
            lo, hi = cols
            return grouped[:, lo * PACK : hi * PACK].rearrange("p (c i j) -> p c j i", i=NEAR, j=PACK)

        def quantize(operand, grouped, cols):
            lo, hi = cols
            nc.vector.quantize_mx(
                out=operand[0][:, lo:hi].bitcast(FP8X4),
                scales=operand[1][:, lo:hi],
                in_=grouped[:, lo * PACK : hi * PACK],
            )

        def product(bank, stationary, m, moving, cols):
            lo, hi = cols
            acc = bank[:, : hi - lo]
            nc.tensor.matmul_mx(
                out=acc,
                lhsT=stationary[0][:, m * P : (m + 1) * P].bitcast(FP8X4),
                lhsT_scale=stationary[1][:, m * P : (m + 1) * P],
                rhs=moving[0][:, lo:hi].bitcast(FP8X4),
                rhs_scale=moving[1][:, lo:hi],
                start=True,
                stop=True,
            )
            return acc

        w_grouped = grouped_tile("w", H)
        wa_mx = mx_operand("wa", H)
        wb_mx = mx_operand("wb", N)

        def interleave_weights(stage, cols):
            rows = stage[cols].rearrange("p j (c i) -> p c j i", i=NEAR)
            nc.scalar.activation(grouped_view(w_grouped, cols), rows, COPY)

        def freed(stage, start):
            return stage.rearrange("p j n -> p (j n)")[:, start : start + H]

        ra = [
            freed(wa_stage[UPPER], 0),
            freed(wb_stage[UPPER], 0),
            freed(wb_stage[UPPER], H),
            freed(wb_stage[LOWER], H),
        ]

        def project(t, cols, bank):
            lo, hi = cols
            nc.scalar.activation(ra[t][:, lo:hi], product(bank, xa, t, wa_mx, cols), RELU)

        def scatter(t, cols):
            lo, hi = cols
            entries = slot_sb[:, lo // PER_COLUMN : hi // PER_COLUMN]
            nc.vector.tensor_copy(pages[t % 2][:].indirect(entries), ra[t][:, lo:hi])

        interleave_weights(wa_stage, LOWER)
        quantize(wa_mx, w_grouped, LOWER)
        deal_scales()
        gather_words(offs_sb, xa_words)
        gather_words(two_sb, xb_words)
        interleave_weights(wa_stage, UPPER)
        quantize(wa_mx, w_grouped, UPPER)
        project(0, LOWER, ring_bank())
        scatter(0, LOWER)
        project(0, UPPER, eighth_bank())
        interleave_weights(wb_stage, UPPER)
        quantize(wb_mx, w_grouped, UPPER)
        project(1, (0, H), ring_bank())
        scatter(0, UPPER)
        interleave_weights(wb_stage, LOWER)
        for t in range(2, PACK):
            project(t, (0, H), ring_bank())

        turned = eighth_bank()
        nc.tensor.transpose(turned[:, :P], gain_rows[:], identity[:])
        gains = wb_stage[LOWER][:, 0, : 2 * PACK]
        nc.scalar.activation(gains, turned[:, : 2 * PACK], COPY)

        z_rows = keep.tile([P, PACK * U], BF16, name="z_rows", align_bytes=64)

        def weigh_page(t, c0, c1):
            nc.scalar.activation(
                z_rows[:].rearrange("p (c t n) -> p c t n", t=PACK, n=P)[:, c0:c1, t, :],
                pages[t % 2][:, c0 * P : c1 * P].rearrange("p (c n) -> p c n", n=P),
                COPY,
                scale=gains[:, t : t + 1],
            )

        z2_grouped = grouped_tile("z2", N)
        z2_mx = mx_operand("z2", N)

        def make_z2(cols):
            lo, hi = cols
            rows = keep.tile([P, PACK, hi - lo], BF16, name="z2_rows%d" % lo, align_bytes=64)
            for t in range(PACK):
                acc = product(ring_bank(), xb, t, wb_mx, cols)
                nc.scalar.activation(rows[:, t, :], acc, COPY, scale=gains[:, PACK + t : PACK + t + 1])
            nc.scalar.copy(grouped_view(z2_grouped, cols), rows[:].rearrange("p t (c i) -> p c t i", i=NEAR))

        scatter(1, (0, H))
        quantize(wb_mx, w_grouped, LOWER)
        weigh_page(0, 0, CHUNKS)
        make_z2(UPPER)
        scatter(2, (0, H))
        weigh_page(1, 0, CHUNKS)
        make_z2(LOWER)
        scatter(3, (0, H))
        weigh_page(2, 0, CHUNKS)

        z_grouped, z_mx = {}, {}

        def interleave_z(group):
            c0, c1 = group
            weigh_page(PACK - 1, c0, c1)
            z_grouped[group] = grouped_tile("z_from%d" % c0, (c1 - c0) * P)
            z_mx[group] = mx_operand("z_from%d" % c0, (c1 - c0) * P)
            nc.vector.tensor_copy(
                z_grouped[group][:].rearrange("p (c n i t) -> p c n t i", n=P // NEAR, i=NEAR, t=PACK),
                z_rows[:, PACK * c0 * P : PACK * c1 * P].rearrange(
                    "p (c t n i) -> p c n t i", t=PACK, n=P // NEAR, i=NEAR
                ),
            )

        def quantize_z(group):
            quantize(z_mx[group], z_grouped[group], (0, (group[1] - group[0]) * P))

        quantize(z2_mx, z2_grouped, UPPER)
        interleave_z(TAIL_GROUPS[0])
        quantize(z2_mx, z2_grouped, LOWER)
        quantize_z(TAIL_GROUPS[0])
        interleave_z(TAIL_GROUPS[1])
        for group, following in zip(TAIL_GROUPS[1:], TAIL_GROUPS[2:]):
            interleave_z(following)
            quantize_z(group)
        quantize_z(TAIL_GROUPS[-1])

        for group in TAIL_GROUPS:
            for c in range(*group):
                for lo, hi in (LOWER, UPPER) if c in SPLIT_CHUNKS else ((0, N),):
                    acc = product(ring_bank(), z_mx[group], c - group[0], z2_mx, (lo, hi))
                    result = keep.tile([P, hi - lo], F32, name="result%d_%d" % (c, lo))
                    if (c, lo) in VECTOR_PIECES:
                        nc.vector.tensor_scalar(result[:], acc, OUT_SCALE, None, MULT)
                    else:
                        nc.scalar.activation(result[:], acc, COPY, scale=OUT_SCALE)
                    nc.sync.dma_start(out[c * P : (c + 1) * P, lo:hi], result[:])
